import numpy as np
import ml_dtypes


def mxq(x, axis, fmt="e4m3"):
    dtype, down = {"e4m3": (ml_dtypes.float8_e4m3fn, 7), "e5m2": (ml_dtypes.float8_e5m2, 14)}[fmt]
    v = np.moveaxis(np.asarray(x, np.float32).astype(ml_dtypes.bfloat16).astype(np.float64), axis, -1)
    blocks = v.reshape(v.shape[:-1] + (-1, 32))
    amax = np.abs(blocks).max(-1, keepdims=True)
    byte = np.maximum(np.where(amax > 0, np.frexp(amax)[1] - 1 + 127, 0) - down, 1)
    scale = np.exp2(byte - 127.0)
    codes = (blocks / scale).astype(np.float32).astype(dtype).astype(np.float64)
    return np.moveaxis((codes * scale).reshape(v.shape), -1, axis)


WIDE = False


def mx_kscale(k):
    if not WIDE:
        return np.ones(k)
    levels = np.array([10, -10, 5, -5, 0])
    if k % 512:
        return np.exp2(np.random.permutation(np.resize(levels, k // 32))).repeat(32)
    a = np.empty((k // 512, 16))
    for p in range(k // 512):
        a[p, :8] = np.random.permutation(np.resize(levels, 8))
        for g in range(8):
            far = levels[np.abs(levels - a[p, g]) >= 10]
            a[p, g + 8] = far[np.random.randint(len(far))]
    return np.exp2(a.ravel()).repeat(32)


def f64(x):
    return np.asarray(x).astype(np.float64)


def striped(idx):
    return np.tile(idx.reshape(-1, 16).T, (8, 1)).astype(np.uint16)


def unstriped(offs):
    return offs[:16].T.reshape(-1).astype(np.int64)


def striped8(idx):
    return np.concatenate([x.reshape(-1, 16).T for x in idx]).astype(np.uint16)


def runs(offs, k):
    lists = np.stack([offs[16 * r : 16 * r + 16].T.reshape(-1) for r in range(8)]).astype(np.int64)
    return lists[np.arange(k) % 512 // 64]


def pack_weight(w):
    k, n = w.shape
    w = f64(np.asarray(w, np.float32).astype(ml_dtypes.bfloat16)).reshape(k // 32, 32, n)
    amax = np.abs(w).max(1)
    byte = np.clip(np.where(amax > 0, np.frexp(amax)[1] - 1 + 127 - 7, 1), 1, 254)
    scaled = (w * np.exp2(127.0 - byte)[:, None, :]).reshape(k, n).astype(np.float32)
    words = np.ascontiguousarray(scaled.reshape(k // 512, 128, 4, n).transpose(0, 1, 3, 2)).astype(ml_dtypes.float8_e4m3fn).view(np.uint8)
    return words, np.ascontiguousarray(byte.astype(np.uint8).reshape(k // 512, 16, n))


def unpack_weight(words, scales):
    g, p, n, _ = words.shape
    vals = np.ascontiguousarray(words).view(ml_dtypes.float8_e4m3fn).astype(np.float64) * np.repeat(np.exp2(scales.astype(np.float64) - 127.0), 8, axis=1)[..., None]
    return vals.transpose(0, 1, 3, 2).reshape(g * 512, n)


E2M1 = np.array([0.0, 0.5, 1.0, 1.5, 2.0, 3.0, 4.0, 6.0, -0.0, -0.5, -1.0, -1.5, -2.0, -3.0, -4.0, -6.0])


def pack_fp4(w):
    k, n = w.shape
    w = f64(np.asarray(w, np.float32).astype(ml_dtypes.bfloat16)).reshape(k // 32, 32, n)
    amax = np.abs(w).max(1)
    mant, ex = np.frexp(amax / 6.0)
    byte = np.clip(np.where(amax > 0, np.where(mant > 0.5, ex, ex - 1) + 127, 1), 1, 254)
    scaled = (w * np.exp2(127.0 - byte)[:, None, :]).reshape(k, n).astype(np.float32)
    c = np.ascontiguousarray(scaled.reshape(k // 512, 128, 4, n).transpose(0, 1, 3, 2)).astype(ml_dtypes.float4_e2m1fn).view(np.uint8) & 0xF
    words = (c[..., 0::2] | (c[..., 1::2] << 4)).reshape(k // 512, 128, 2 * n)
    return np.ascontiguousarray(words), np.ascontiguousarray(byte.astype(np.uint8).reshape(k // 512, 16, n))


def unpack_fp4(words, scales):
    g, _, n = scales.shape
    words = np.ascontiguousarray(words).reshape(g, 128, n, 2)
    nib = np.empty((g, 128, n, 4), np.uint8)
    nib[..., 0::2] = words & 0xF
    nib[..., 1::2] = words >> 4
    vals = E2M1[nib] * np.repeat(np.exp2(scales.astype(np.float64) - 127.0), 8, axis=1)[..., None]
    return vals.transpose(0, 1, 3, 2).reshape(g * 512, n)


def sigmoid(v):
    return 1.0 / (1.0 + np.exp(-np.maximum(v, -700.0)))

def planes(y):
    n, m = y.shape
    v = y.astype(np.float32).astype(ml_dtypes.bfloat16).astype(np.float64).reshape(n // 32, 32, m)
    top = np.abs(v).max(1)
    byte = np.clip(np.where(top > 0, np.frexp(top)[1] - 1 + 127 - 7, 1), 1, 254)
    codes = (v * np.exp2(127.0 - byte)[:, None, :]).reshape(n, m).astype(np.float32).astype(ml_dtypes.float8_e4m3fn).view(np.uint8)
    words = codes.reshape(n // 512, 128, 4, m).transpose(0, 1, 3, 2)
    return np.ascontiguousarray(words), np.ascontiguousarray(byte.astype(np.uint8).reshape(n // 512, 16, m))


K, T, S, N, G, H, W = 512, 2048, 512, 512, 2048, 512, 256


def setup_inputs():
    n = np.random.standard_normal
    s = mx_kscale(K)[:, None]
    u = mx_kscale(S)
    packed_xT = pack_weight(n((K, T)) * s)
    packed_dT = pack_weight(n((K, G)) / s)
    packed_w1 = pack_fp4(n((H, N)) / np.sqrt(H) / u[:, None])
    perm = np.random.permutation(S)
    return {
        "x_words": packed_xT[0],
        "x_scales": packed_xT[1],
        "d_words": packed_dT[0],
        "d_scales": packed_dT[1],
        "sl": np.random.uniform(1.5, 3.0, (H, 1)).astype(np.float32),
        "th": (0.5 * n((H, 1))).astype(np.float32),
        "gn": (np.random.uniform(0.5, 1.5, (H, 1)) * u[:, None]).astype(np.float32),
        "w1_words": packed_w1[0],
        "w1_scales": packed_w1[1],
        "offs": striped(np.random.permutation(T)[:S]),
        "k1": striped8(np.random.randint(0, G, (8, H))),
        "n1": striped8(np.stack([np.random.permutation(S) for _ in range(8)])),
        "n2": striped8(np.stack([np.random.permutation(S) for _ in range(8)])),
        "n3": striped(perm[:W]),
        "n4": striped(perm[W:]),
    }


def reference(x_words, x_scales, d_words, d_scales, sl, th, gn, w1_words, w1_scales, offs, k1, n1, n2, n3, n4):
    d_k1 = unpack_weight(d_words, d_scales)[np.arange(K)[:, None], runs(k1, K)]
    xq = unpack_weight(x_words, x_scales)[:, unstriped(offs)]
    h = 0.0625 * (d_k1.T @ xq)
    sg = sigmoid(f64(sl) * (h[np.arange(H)[:, None], runs(n1, H)] - f64(th)))
    z = f64(gn) * (1.5 * (h * (sg - (sg[np.arange(H)[:, None], runs(n2, H)]))))
    h2 = unpack_fp4(w1_words, w1_scales).T @ mxq(z, 0, "e4m3")
    pa = h2[:, unstriped(n3)]
    pb = h2[:, unstriped(n4)]
    rb = np.maximum(0.5 * pa, pb)
    ra = pb - pa
    ds = np.zeros((N, S))
    ds[:, unstriped(n3)] = ra
    out = ds.copy()
    out[:, unstriped(n4)] = rb
    return (out,) + planes(out)

@@ -1,0 +1,220 @@
+from contextlib import ExitStack
+
+import concourse.mybir as mybir
+
+F32 = mybir.dt.float32
+BF16 = mybir.dt.bfloat16
+I32 = mybir.dt.int32
+U32 = mybir.dt.uint32
+U16 = mybir.dt.uint16
+U8 = mybir.dt.uint8
+FP8X4 = mybir.dt.float8_e4m3fn_x4
+FP4X4 = mybir.dt.float4_e2m1fn_x4
+ALU = mybir.AluOpType
+ACT = mybir.ActivationFunctionType
+
+P = 128
+PACK = 4
+T = 2048
+S = 512
+HALF = 256
+FLOPS = 2 * 2 * 512 * 512 * 512
+
+
+def tile_picked_pqlayedblift_none_po_kernel(
+    tc, x_words, x_scales, d_words, d_scales, sl, th, gn, w1_words, w1_scales,
+    offs, k1, n1, n2, n3, n4, out_0, out_1, out_2,
+):
+    nc = tc.nc
+    with ExitStack() as ctx:
+        lists = ctx.enter_context(tc.tile_pool(name="lists", bufs=1))
+        sb = ctx.enter_context(tc.tile_pool(name="sb", bufs=1))
+        ps = ctx.enter_context(tc.psum_pool(name="ps", bufs=1))
+
+        def new(name, width, dtype, tag=None):
+            return sb.tile([P, width], dtype, name=name, tag=tag or name, align_bytes=64)
+
+        def load_list(name, src):
+            tile = lists.tile([P, src.shape[1]], U16, name=name)
+            nc.sync.dma_start(tile[:], src)
+            return tile
+
+        def half(a):
+            return slice(a * HALF, (a + 1) * HALF)
+
+        def half_list(tile, a):
+            return tile[:, a * HALF // 16 : (a + 1) * HALF // 16]
+
+        d_sc = new("d_sc", T, U8)
+        x_sc = new("x_sc", T, U8)
+        d_plane = new("d_plane", S, U8)
+        nc.gpsimd.memset(d_sc[:].bitcast(I32), 0)
+        nc.vector.memset(x_sc[:].bitcast(I32), 0)
+        nc.vector.memset(d_plane[:].bitcast(I32), 0)
+
+        k1_t = load_list("k1", k1)
+        offs_t = load_list("offs", offs)
+        nc.sync.dma_start(d_sc[0:P:8, :].bitcast(I32), d_scales[0].bitcast(I32))
+        for q in range(4):
+            nc.sync.dma_start(x_sc[32 * q : 32 * q + 4, :].bitcast(I32), x_scales[0, 4 * q : 4 * q + 4, :].bitcast(I32))
+        d_w = new("d_w", T, U32)
+        x_w = new("x_w", T, U32)
+        w_raw = new("w_raw", 2 * S, U8)
+        nc.sync.dma_start(d_w[:].bitcast(I32), d_words[0].rearrange("p c r -> p (c r)").bitcast(I32))
+        nc.sync.dma_start(w_raw[:].bitcast(I32), w1_words[0].bitcast(I32))
+        n1_t = load_list("n1", n1)
+        nc.sync.dma_start(x_w[:].bitcast(I32), x_words[0].rearrange("p c r -> p (c r)").bitcast(I32))
+        n2_t = load_list("n2", n2)
+        n3_t = load_list("n3", n3)
+        n4_t = load_list("n4", n4)
+
+        sl_t = new("sl_t", PACK, F32)
+        th_t = new("th_t", PACK, F32)
+        gn_t = new("gn_t", PACK, F32)
+        for tile, src in ((sl_t, sl), (th_t, th), (gn_t, gn)):
+            nc.gpsimd.dma_start(tile[:], src.rearrange("(p t) o -> p (t o)", t=PACK))
+        bias = new("bias", PACK, F32)
+        gain = new("gain", PACK, F32)
+        slth = new("slth", PACK, F32)
+        nc.gpsimd.tensor_tensor(slth[:], sl_t[:], th_t[:], ALU.mult)
+        nc.gpsimd.tensor_scalar(bias[:], slth[:], -1.0, 0.0, ALU.mult, ALU.add)
+        nc.gpsimd.tensor_scalar(gain[:], gn_t[:], -1.5, 0.0, ALU.mult, ALU.add)
+
+        w_codes = new("w_codes", 2 * S, U8)
+        nc.scalar.copy(w_codes[:].bitcast(U16).rearrange("p (t m) -> p m t", t=PACK), w_raw[:].bitcast(U16).rearrange("p (m t) -> p m t", t=PACK))
+
+        d_sc_g = new("d_sc_g", S, U8, tag="undealt")
+        nc.vector.tensor_copy(d_sc_g[:], d_sc[:].indirect(k1_t[:]))
+        d_sc_d = new("d_sc_d", S, U8)
+        nc.vector.tensor_copy(d_sc_d[:].rearrange("p (t m) -> p m t", t=PACK), d_sc_g[:].rearrange("p (m t) -> p m t", t=PACK))
+        for q in range(4):
+            nc.scalar.dma_start(d_plane[32 * q : 32 * q + 4, :].bitcast(I32), d_sc_d[32 * q : 32 * q + 32 : 8, :].bitcast(I32))
+        x_plane = new("x_plane", S, U8)
+        nc.vector.tensor_copy(x_plane[:], x_sc[:].indirect(offs_t[:]))
+        d_g = new("d_g", S, U32)
+        nc.vector.tensor_copy(d_g[:], d_w[:].indirect(k1_t[:]))
+        d_codes = new("d_codes", S, U32)
+        nc.vector.tensor_copy(d_codes[:].rearrange("p (t m) -> p m t", t=PACK), d_g[:].rearrange("p (m t) -> p m t", t=PACK))
+
+        w_sc = new("w_sc", S, U8, tag="undealt")
+        nc.gpsimd.memset(w_sc[:].bitcast(I32), 0)
+        for q in range(4):
+            nc.sync.dma_start(w_sc[32 * q : 32 * q + 4, :].bitcast(I32), w1_scales[0, 4 * q : 4 * q + 4, :].bitcast(I32))
+
+        x_codes = [new(f"x_codes{a}", HALF, U32) for a in range(2)]
+        h = [new(f"h{t}", 2 * S, F32) for t in range(PACK)]
+        banks = {}
+        for a in range(2):
+            nc.vector.tensor_copy(x_codes[a][:], x_w[:].indirect(half_list(offs_t, a)))
+        for t in range(PACK):
+            for a in range(2):
+                bank = ps.tile([P, HALF], F32, name=f"h_bank{t}{a}", tag=f"bank{t}{a}")
+                banks[t, a] = bank
+                nc.tensor.matmul_mx(
+                    out=bank[:], lhsT=d_codes[:, t * P : (t + 1) * P].bitcast(FP8X4), lhsT_scale=d_plane[:, t * P : (t + 1) * P],
+                    rhs=x_codes[a][:].bitcast(FP8X4), rhs_scale=x_plane[:, half(a)], start=True, stop=True)
+                nc.vector.tensor_scalar(h[t][:, half(a)], banks[t, a][:], 0.0625, None, ALU.mult)
+
+        w_plane = new("w_plane", S, U8)
+        nc.vector.tensor_copy(w_plane[:].rearrange("p (t m) -> p m t", t=PACK), w_sc[:].rearrange("p (m t) -> p m t", t=PACK))
+
+        sg = [new(f"sg{t}", 2 * S, F32) for t in range(PACK)]
+        other = [new(f"other{t}", S, F32) for t in range(PACK)]
+        diff = [new(f"diff{t}", S, F32) for t in range(PACK)]
+        z_rows = new("z_rows", PACK * S, BF16)
+        for t in range(PACK):
+            nc.scalar.activation(sg[t][:, :S], h[t][:].indirect(n1_t[:]), ACT.Sigmoid,
+                                 bias=bias[:, t : t + 1], scale=sl_t[:, t : t + 1])
+
+        def gate(t, lo, hi, on_vector):
+            cols = slice(lo, hi)
+            picks = sg[t][:].indirect(n2_t[:, lo // 16 : hi // 16])
+            if on_vector:
+                nc.vector.tensor_copy(other[t][:, cols], sg[t][:, cols])
+                nc.vector.tensor_tensor(diff[t][:, cols], picks, other[t][:, cols], ALU.subtract)
+            else:
+                nc.scalar.activation(other[t][:, cols], picks, ACT.Copy)
+                nc.vector.tensor_tensor(diff[t][:, cols], other[t][:, cols], sg[t][:, cols], ALU.subtract)
+            nc.vector.scalar_tensor_tensor(z_rows[:, t * S + lo : t * S + hi], diff[t][:, cols], gain[:, t : t + 1],
+                                           h[t][:, cols], ALU.mult, ALU.mult)
+
+        gate(0, 0, S, True)
+        gate(1, 0, HALF, True)
+        gate(2, 0, HALF, False)
+        gate(3, 0, HALF, False)
+        for t in range(1, PACK):
+            gate(t, HALF, S, False)
+
+        def quantise(name, rows, splits):
+            codes = new(f"{name}_codes", S, U32)
+            plane = new(f"{name}_plane", S, U8)
+            woven = [new(f"{name}_woven{a}", PACK * HALF, BF16) for a in range(2)]
+            for a in range(2):
+                src = rows[:].rearrange("p (t j) -> p j t", t=PACK)[:, half(a), :]
+                dst = woven[a][:].rearrange("p (j t) -> p j t", t=PACK)
+                cut = splits[a]
+                if cut > 0:
+                    nc.vector.tensor_copy(dst[:, :cut, :], src[:, :cut, :])
+                if cut < HALF:
+                    nc.scalar.copy(dst[:, cut:, :], src[:, cut:, :])
+            for a in range(2):
+                nc.vector.quantize_mx(codes[:, half(a)].bitcast(FP8X4), plane[:, half(a)], woven[a][:])
+            return codes, plane
+
+        z_codes, z_plane = quantise("z", z_rows, (0, HALF))
+
+        h2 = [new(f"h2{t}", S, F32, tag=f"row{t}") for t in range(PACK)]
+        for t in range(PACK):
+            for a in range(2):
+                bank = ps.tile([P, HALF], F32, name=f"h2_bank{t}{a}", tag=f"bank{t}{a}")
+                banks[t, a] = bank
+                nc.tensor.matmul_mx(
+                    out=bank[:], lhsT=w_codes[:, 2 * t * P : 2 * (t + 1) * P].bitcast(FP4X4), lhsT_scale=w_plane[:, t * P : (t + 1) * P],
+                    rhs=z_codes[:, half(a)].bitcast(FP8X4), rhs_scale=z_plane[:, half(a)], start=True, stop=True)
+
+        npa = [new(f"npa{t}", HALF, F32) for t in range(PACK)]
+        pb = [new(f"pb{t}", HALF, F32) for t in range(PACK)]
+        rb = [new(f"rb{t}", HALF, F32) for t in range(PACK)]
+        res = {}
+        y_rows = new("y_rows", PACK * S, BF16)
+        out_rows = out_0.rearrange("(p t) j -> p t j", t=PACK)
+
+        def fetch(t):
+            nc.scalar.copy(h2[t][:, half(0)], banks[t, 0][:])
+            if t == 0:
+                nc.vector.tensor_copy(h2[t][:, half(1)], banks[t, 1][:])
+            else:
+                nc.scalar.copy(h2[t][:, half(1)], banks[t, 1][:])
+            nc.scalar.activation(npa[t][:], h2[t][:].indirect(n3_t[:]), ACT.Copy, scale=-1.0)
+            nc.vector.tensor_copy(pb[t][:], h2[t][:].indirect(n4_t[:]))
+            nc.vector.scalar_tensor_tensor(rb[t][:], npa[t][:], -0.5, pb[t][:], ALU.mult, ALU.max)
+
+        def put_a(t):
+            nc.vector.tensor_tensor(res[t][:].indirect(n3_t[:]), pb[t][:], npa[t][:], ALU.add)
+
+        def put_b(t):
+            nc.scalar.activation(res[t][:].indirect(n4_t[:]), rb[t][:], ACT.Copy)
+
+        def finish(t):
+            nc.sync.dma_start(out_rows[:, t, :], res[t][:])
+            nc.vector.tensor_copy(y_rows[:, t * S : (t + 1) * S], res[t][:])
+
+        for t in (0, 2):
+            fetch(t)
+            fetch(t + 1)
+            res[t] = new(f"res{t}", S, F32, tag=f"row{t + 1}")
+            res[t + 1] = new(f"res{t + 1}", S, F32, tag=f"row{t}")
+            put_a(t)
+            put_b(t + 1)
+            put_a(t + 1)
+            put_b(t)
+            finish(t + 1)
+            finish(t)
+
+        y_codes, y_plane = quantise("y", y_rows, (160, 160))
+        words_out = out_1[0].rearrange("p c r -> p (c r)").bitcast(I32)
+        for a in range(2):
+            nc.sync.dma_start(words_out[:, half(a)], y_codes[:, half(a)].bitcast(I32))
+        for q in range(4):
+            eng = nc.scalar if q % 2 else nc.sync
+            eng.dma_start(out_2[0, 4 * q : 4 * q + 4, :].bitcast(I32), y_plane[32 * q : 32 * q + 4, :].bitcast(I32))

@@ -52,6 +52,11 @@ def tile_picked_pqlayedblift_none_po_kernel(
         nc.vector.memset(x_sc[:].bitcast(I32), 0)
         nc.vector.memset(d_plane[:].bitcast(I32), 0)
 
+        warm_in = new("warm_in", 1, F32)
+        warm_out = new("warm_out", 1, F32)
+        nc.vector.memset(warm_in[:], 0.0)
+        nc.scalar.activation(warm_out[:], warm_in[:], ACT.Sigmoid)
+
         k1_t = load_list("k1", k1)
         offs_t = load_list("offs", offs)
         nc.sync.dma_start(d_sc[0:P:8, :].bitcast(I32), d_scales[0].bitcast(I32))

@@ -94,81 +94,97 @@ def tile_picked_pqlayedblift_none_po_kernel(
         nc.vector.tensor_copy(d_sc_d[:].rearrange("p (t m) -> p m t", t=PACK), d_sc_g[:].rearrange("p (m t) -> p m t", t=PACK))
         for q in range(4):
             nc.scalar.dma_start(d_plane[32 * q : 32 * q + 4, :].bitcast(I32), d_sc_d[32 * q : 32 * q + 32 : 8, :].bitcast(I32))
-        x_plane = new("x_plane", S, U8)
+        x_plane = new("x_plane", S, U8, tag="undealt")
         nc.vector.tensor_copy(x_plane[:], x_sc[:].indirect(offs_t[:]))
         d_g = new("d_g", S, U32)
         nc.vector.tensor_copy(d_g[:], d_w[:].indirect(k1_t[:]))
         d_codes = new("d_codes", S, U32)
         nc.vector.tensor_copy(d_codes[:].rearrange("p (t m) -> p m t", t=PACK), d_g[:].rearrange("p (m t) -> p m t", t=PACK))
 
-        w_sc = new("w_sc", S, U8, tag="undealt")
+        x_codes = new("x_codes", S, U32)
+        h = [new(f"h{t}", 2 * S, F32) for t in range(PACK)]
+        for a in range(2):
+            nc.vector.tensor_copy(x_codes[:, half(a)], x_w[:].indirect(half_list(offs_t, a)))
+
+        w_sc = new("w_sc", S, U8, tag="x_w")
         nc.gpsimd.memset(w_sc[:].bitcast(I32), 0)
         for q in range(4):
             nc.sync.dma_start(w_sc[32 * q : 32 * q + 4, :].bitcast(I32), w1_scales[0, 4 * q : 4 * q + 4, :].bitcast(I32))
 
-        x_codes = [new(f"x_codes{a}", HALF, U32) for a in range(2)]
-        h = [new(f"h{t}", 2 * S, F32) for t in range(PACK)]
-        banks = {}
-        for a in range(2):
-            nc.vector.tensor_copy(x_codes[a][:], x_w[:].indirect(half_list(offs_t, a)))
+        def first_product(t, lo, hi, on_vector):
+            bank = ps.tile([P, hi - lo], F32, name=f"h_bank{t}_{lo}", tag=f"bank{t}{lo // HALF}")
+            nc.tensor.matmul_mx(
+                out=bank[:], lhsT=d_codes[:, t * P : (t + 1) * P].bitcast(FP8X4), lhsT_scale=d_plane[:, t * P : (t + 1) * P],
+                rhs=x_codes[:, lo:hi].bitcast(FP8X4), rhs_scale=x_plane[:, lo:hi], start=True, stop=True)
+            if on_vector:
+                nc.vector.tensor_scalar(h[t][:, lo:hi], bank[:], 0.0625, None, ALU.mult)
+            else:
+                nc.scalar.activation(h[t][:, lo:hi], bank[:], ACT.Copy, scale=0.0625)
+
+        sg = [new(f"sg{t}", 2 * S, F32) for t in range(PACK)]
+
+        def sigmoid(t):
+            nc.scalar.activation(sg[t][:, :S], h[t][:].indirect(n1_t[:]), ACT.Sigmoid,
+                                 bias=bias[:, t : t + 1], scale=sl_t[:, t : t + 1])
+
+        first_product(0, 0, HALF, False)
+        first_product(1, 0, HALF, False)
+        first_product(0, HALF, S, True)
+        first_product(1, HALF, S, True)
+        first_product(2, 0, S, True)
+        first_product(3, 0, S, True)
         for t in range(PACK):
-            for a in range(2):
-                bank = ps.tile([P, HALF], F32, name=f"h_bank{t}{a}", tag=f"bank{t}{a}")
-                banks[t, a] = bank
-                nc.tensor.matmul_mx(
-                    out=bank[:], lhsT=d_codes[:, t * P : (t + 1) * P].bitcast(FP8X4), lhsT_scale=d_plane[:, t * P : (t + 1) * P],
-                    rhs=x_codes[a][:].bitcast(FP8X4), rhs_scale=x_plane[:, half(a)], start=True, stop=True)
-                nc.vector.tensor_scalar(h[t][:, half(a)], banks[t, a][:], 0.0625, None, ALU.mult)
+            sigmoid(t)
 
         w_plane = new("w_plane", S, U8)
         nc.vector.tensor_copy(w_plane[:].rearrange("p (t m) -> p m t", t=PACK), w_sc[:].rearrange("p (m t) -> p m t", t=PACK))
 
-        sg = [new(f"sg{t}", 2 * S, F32) for t in range(PACK)]
-        other = [new(f"other{t}", S, F32) for t in range(PACK)]
-        diff = [new(f"diff{t}", S, F32) for t in range(PACK)]
         z_rows = new("z_rows", PACK * S, BF16)
-        for t in range(PACK):
-            nc.scalar.activation(sg[t][:, :S], h[t][:].indirect(n1_t[:]), ACT.Sigmoid,
-                                 bias=bias[:, t : t + 1], scale=sl_t[:, t : t + 1])
+        z_view = z_rows[:].rearrange("p (a t j) -> p t a j", a=2, t=PACK)
 
-        def gate(t, lo, hi, on_vector):
-            cols = slice(lo, hi)
-            picks = sg[t][:].indirect(n2_t[:, lo // 16 : hi // 16])
-            if on_vector:
-                nc.vector.tensor_copy(other[t][:, cols], sg[t][:, cols])
-                nc.vector.tensor_tensor(diff[t][:, cols], picks, other[t][:, cols], ALU.subtract)
-            else:
-                nc.scalar.activation(other[t][:, cols], picks, ACT.Copy)
-                nc.vector.tensor_tensor(diff[t][:, cols], other[t][:, cols], sg[t][:, cols], ALU.subtract)
-            nc.vector.scalar_tensor_tensor(z_rows[:, t * S + lo : t * S + hi], diff[t][:, cols], gain[:, t : t + 1],
-                                           h[t][:, cols], ALU.mult, ALU.mult)
+        def halves(ap):
+            return ap.rearrange("p (a j) -> p a j", j=HALF)
 
-        gate(0, 0, S, True)
-        gate(1, 0, HALF, True)
-        gate(2, 0, HALF, False)
-        gate(3, 0, HALF, False)
-        for t in range(1, PACK):
-            gate(t, HALF, S, False)
+        def scale_rows(t, lo, hi, diff):
+            nc.vector.scalar_tensor_tensor(z_view[:, t, lo // HALF : hi // HALF, :], halves(diff), gain[:, t : t + 1], halves(h[t][:, lo:hi]), ALU.mult, ALU.mult)
+
+        for t, width in ((0, S), (1, HALF)):
+            same = new(f"same{t}", width, F32, tag="operand")
+            diff = new(f"diff{t}", width, F32)
+            nc.vector.tensor_copy(same[:], sg[t][:, :width])
+            nc.vector.tensor_tensor(diff[:], sg[t][:].indirect(n2_t[:, : width // 16]), same[:], ALU.subtract)
+            scale_rows(t, 0, width, diff[:])
+        rest = ((2, 0), (3, 0), (1, 1), (2, 1), (3, 1))
+        picked = new("picked", len(rest) * HALF, F32)
+        diffs = new("diffs", len(rest) * HALF, F32, tag="operand")
+        for i, (t, a) in enumerate(rest):
+            nc.scalar.activation(picked[:, half(i)], sg[t][:].indirect(half_list(n2_t, a)), ACT.Copy)
+            nc.vector.tensor_tensor(diffs[:, half(i)], picked[:, half(i)], sg[t][:, half(a)], ALU.subtract)
+            scale_rows(t, a * HALF, (a + 1) * HALF, diffs[:, half(i)])
+
+        def walk(ap):
+            return ap.rearrange("p (c i) t -> p c t i", i=4)
 
         def quantise(name, rows, splits):
             codes = new(f"{name}_codes", S, U32)
             plane = new(f"{name}_plane", S, U8)
             woven = [new(f"{name}_woven{a}", PACK * HALF, BF16) for a in range(2)]
             for a in range(2):
-                src = rows[:].rearrange("p (t j) -> p j t", t=PACK)[:, half(a), :]
+                src = rows[a]
                 dst = woven[a][:].rearrange("p (j t) -> p j t", t=PACK)
                 cut = splits[a]
                 if cut > 0:
-                    nc.vector.tensor_copy(dst[:, :cut, :], src[:, :cut, :])
+                    nc.vector.tensor_copy(walk(dst[:, :cut, :]), walk(src[:, :cut, :]))
                 if cut < HALF:
-                    nc.scalar.copy(dst[:, cut:, :], src[:, cut:, :])
+                    nc.scalar.copy(walk(dst[:, cut:, :]), walk(src[:, cut:, :]))
             for a in range(2):
                 nc.vector.quantize_mx(codes[:, half(a)].bitcast(FP8X4), plane[:, half(a)], woven[a][:])
             return codes, plane
 
-        z_codes, z_plane = quantise("z", z_rows, (0, HALF))
+        z_codes, z_plane = quantise("z", [z_rows[:, a * PACK * HALF : (a + 1) * PACK * HALF].rearrange("p (t j) -> p j t", t=PACK) for a in range(2)], (0, 160))
 
         h2 = [new(f"h2{t}", S, F32, tag=f"row{t}") for t in range(PACK)]
+        banks = {}
         for t in range(PACK):
             for a in range(2):
                 bank = ps.tile([P, HALF], F32, name=f"h2_bank{t}{a}", tag=f"bank{t}{a}")
@@ -191,7 +207,10 @@ def tile_picked_pqlayedblift_none_po_kernel(
             else:
                 nc.scalar.copy(h2[t][:, half(1)], banks[t, 1][:])
             nc.scalar.activation(npa[t][:], h2[t][:].indirect(n3_t[:]), ACT.Copy, scale=-1.0)
-            nc.vector.tensor_copy(pb[t][:], h2[t][:].indirect(n4_t[:]))
+            if t < 3:
+                nc.vector.tensor_copy(pb[t][:], h2[t][:].indirect(n4_t[:]))
+            else:
+                nc.scalar.activation(pb[t][:], h2[t][:].indirect(n4_t[:]), ACT.Copy)
             nc.vector.scalar_tensor_tensor(rb[t][:], npa[t][:], -0.5, pb[t][:], ALU.mult, ALU.max)
 
         def put_a(t):
@@ -202,21 +221,28 @@ def tile_picked_pqlayedblift_none_po_kernel(
 
         def finish(t):
             nc.sync.dma_start(out_rows[:, t, :], res[t][:])
-            nc.vector.tensor_copy(y_rows[:, t * S : (t + 1) * S], res[t][:])
+            if t < 3:
+                nc.vector.tensor_copy(y_rows[:, t * S : (t + 1) * S], res[t][:])
+            else:
+                nc.vector.tensor_copy(y_rows[:, t * S : t * S + HALF], res[t][:, half(0)])
+                nc.scalar.copy(y_rows[:, t * S + HALF : (t + 1) * S], res[t][:, half(1)])
 
-        for t in (0, 2):
+        for t in range(PACK):
             fetch(t)
-            fetch(t + 1)
-            res[t] = new(f"res{t}", S, F32, tag=f"row{t + 1}")
-            res[t + 1] = new(f"res{t + 1}", S, F32, tag=f"row{t}")
-            put_a(t)
-            put_b(t + 1)
-            put_a(t + 1)
-            put_b(t)
-            finish(t + 1)
+        for t, slot in enumerate(("row2", "row0", "row1", "npa0")):
+            res[t] = new(f"res{t}", S, F32, tag=slot)
+        put_a(0)
+        put_b(1)
+        put_a(3)
+        put_b(2)
+        put_a(1)
+        put_b(0)
+        put_a(2)
+        put_b(3)
+        for t in (1, 0, 2, 3):
             finish(t)
 
-        y_codes, y_plane = quantise("y", y_rows, (160, 160))
+        y_codes, y_plane = quantise("y", [y_rows[:].rearrange("p (t j) -> p j t", t=PACK)[:, half(a), :] for a in range(2)], (HALF, 96))
         words_out = out_1[0].rearrange("p c r -> p (c r)").bitcast(I32)
         for a in range(2):
             nc.sync.dma_start(words_out[:, half(a)], y_codes[:, half(a)].bitcast(I32))

from contextlib import ExitStack

import concourse.mybir as mybir

F32 = mybir.dt.float32
BF16 = mybir.dt.bfloat16
I32 = mybir.dt.int32
U32 = mybir.dt.uint32
U16 = mybir.dt.uint16
U8 = mybir.dt.uint8
FP8X4 = mybir.dt.float8_e4m3fn_x4
FP4X4 = mybir.dt.float4_e2m1fn_x4
ALU = mybir.AluOpType
ACT = mybir.ActivationFunctionType

P = 128
PACK = 4
T = 2048
S = 512
HALF = 256
FLOPS = 2 * 2 * 512 * 512 * 512


def tile_picked_pqlayedblift_none_po_kernel(
    tc, x_words, x_scales, d_words, d_scales, sl, th, gn, w1_words, w1_scales,
    offs, k1, n1, n2, n3, n4, out_0, out_1, out_2,
):
    nc = tc.nc
    with ExitStack() as ctx:
        lists = ctx.enter_context(tc.tile_pool(name="lists", bufs=1))
        sb = ctx.enter_context(tc.tile_pool(name="sb", bufs=1))
        ps = ctx.enter_context(tc.psum_pool(name="ps", bufs=1))

        def new(name, width, dtype, tag=None):
            return sb.tile([P, width], dtype, name=name, tag=tag or name, align_bytes=64)

        def load_list(name, src):
            tile = lists.tile([P, src.shape[1]], U16, name=name)
            nc.sync.dma_start(tile[:], src)
            return tile

        def half(a):
            return slice(a * HALF, (a + 1) * HALF)

        def half_list(tile, a):
            return tile[:, a * HALF // 16 : (a + 1) * HALF // 16]

        d_sc = new("d_sc", T, U8)
        x_sc = new("x_sc", T, U8)
        d_plane = new("d_plane", S, U8)
        nc.gpsimd.memset(d_sc[:].bitcast(I32), 0)
        nc.vector.memset(x_sc[:].bitcast(I32), 0)
        nc.vector.memset(d_plane[:].bitcast(I32), 0)

        warm_in = new("warm_in", 1, F32)
        warm_out = new("warm_out", 1, F32)
        nc.vector.memset(warm_in[:], 0.0)
        nc.scalar.activation(warm_out[:], warm_in[:], ACT.Sigmoid)

        k1_t = load_list("k1", k1)
        offs_t = load_list("offs", offs)
        nc.sync.dma_start(d_sc[0:P:8, :].bitcast(I32), d_scales[0].bitcast(I32))
        for q in range(4):
            nc.sync.dma_start(x_sc[32 * q : 32 * q + 4, :].bitcast(I32), x_scales[0, 4 * q : 4 * q + 4, :].bitcast(I32))
        d_w = new("d_w", T, U32)
        x_w = new("x_w", T, U32)
        w_raw = new("w_raw", 2 * S, U8)
        nc.sync.dma_start(d_w[:].bitcast(I32), d_words[0].rearrange("p c r -> p (c r)").bitcast(I32))
        nc.sync.dma_start(w_raw[:].bitcast(I32), w1_words[0].bitcast(I32))
        n1_t = load_list("n1", n1)
        nc.sync.dma_start(x_w[:].bitcast(I32), x_words[0].rearrange("p c r -> p (c r)").bitcast(I32))
        n2_t = load_list("n2", n2)
        n3_t = load_list("n3", n3)
        n4_t = load_list("n4", n4)

        sl_t = new("sl_t", PACK, F32)
        th_t = new("th_t", PACK, F32)
        gn_t = new("gn_t", PACK, F32)
        for tile, src in ((sl_t, sl), (th_t, th), (gn_t, gn)):
            nc.gpsimd.dma_start(tile[:], src.rearrange("(p t) o -> p (t o)", t=PACK))
        bias = new("bias", PACK, F32)
        gain = new("gain", PACK, F32)
        slth = new("slth", PACK, F32)
        nc.gpsimd.tensor_tensor(slth[:], sl_t[:], th_t[:], ALU.mult)
        nc.gpsimd.tensor_scalar(bias[:], slth[:], -1.0, 0.0, ALU.mult, ALU.add)
        nc.gpsimd.tensor_scalar(gain[:], gn_t[:], -1.5, 0.0, ALU.mult, ALU.add)

        w_codes = new("w_codes", 2 * S, U8)
        nc.scalar.copy(w_codes[:].bitcast(U16).rearrange("p (t m) -> p m t", t=PACK), w_raw[:].bitcast(U16).rearrange("p (m t) -> p m t", t=PACK))

        d_sc_g = new("d_sc_g", S, U8, tag="undealt")
        nc.vector.tensor_copy(d_sc_g[:], d_sc[:].indirect(k1_t[:]))
        d_sc_d = new("d_sc_d", S, U8)
        nc.vector.tensor_copy(d_sc_d[:].rearrange("p (t m) -> p m t", t=PACK), d_sc_g[:].rearrange("p (m t) -> p m t", t=PACK))
        for q in range(4):
            nc.scalar.dma_start(d_plane[32 * q : 32 * q + 4, :].bitcast(I32), d_sc_d[32 * q : 32 * q + 32 : 8, :].bitcast(I32))
        x_plane = new("x_plane", S, U8, tag="undealt")
        nc.vector.tensor_copy(x_plane[:], x_sc[:].indirect(offs_t[:]))
        d_g = new("d_g", S, U32)
        nc.vector.tensor_copy(d_g[:], d_w[:].indirect(k1_t[:]))
        d_codes = new("d_codes", S, U32)
        nc.vector.tensor_copy(d_codes[:].rearrange("p (t m) -> p m t", t=PACK), d_g[:].rearrange("p (m t) -> p m t", t=PACK))

        x_codes = new("x_codes", S, U32)
        h = [new(f"h{t}", 2 * S, F32) for t in range(PACK)]
        for a in range(2):
            nc.vector.tensor_copy(x_codes[:, half(a)], x_w[:].indirect(half_list(offs_t, a)))

        w_sc = new("w_sc", S, U8, tag="x_w")
        nc.gpsimd.memset(w_sc[:].bitcast(I32), 0)
        for q in range(4):
            nc.sync.dma_start(w_sc[32 * q : 32 * q + 4, :].bitcast(I32), w1_scales[0, 4 * q : 4 * q + 4, :].bitcast(I32))

        def first_product(t, lo, hi, on_vector):
            bank = ps.tile([P, hi - lo], F32, name=f"h_bank{t}_{lo}", tag=f"bank{t}{lo // HALF}")
            nc.tensor.matmul_mx(
                out=bank[:], lhsT=d_codes[:, t * P : (t + 1) * P].bitcast(FP8X4), lhsT_scale=d_plane[:, t * P : (t + 1) * P],
                rhs=x_codes[:, lo:hi].bitcast(FP8X4), rhs_scale=x_plane[:, lo:hi], start=True, stop=True)
            if on_vector:
                nc.vector.tensor_scalar(h[t][:, lo:hi], bank[:], 0.0625, None, ALU.mult)
            else:
                nc.scalar.activation(h[t][:, lo:hi], bank[:], ACT.Copy, scale=0.0625)

        sg = [new(f"sg{t}", 2 * S, F32) for t in range(PACK)]

        def sigmoid(t):
            nc.scalar.activation(sg[t][:, :S], h[t][:].indirect(n1_t[:]), ACT.Sigmoid,
                                 bias=bias[:, t : t + 1], scale=sl_t[:, t : t + 1])

        first_product(0, 0, HALF, False)
        first_product(1, 0, HALF, False)
        first_product(0, HALF, S, True)
        first_product(1, HALF, S, True)
        first_product(2, 0, S, True)
        first_product(3, 0, S, True)
        for t in range(PACK):
            sigmoid(t)

        w_plane = new("w_plane", S, U8)
        nc.vector.tensor_copy(w_plane[:].rearrange("p (t m) -> p m t", t=PACK), w_sc[:].rearrange("p (m t) -> p m t", t=PACK))

        z_rows = new("z_rows", PACK * S, BF16)
        z_view = z_rows[:].rearrange("p (a t j) -> p t a j", a=2, t=PACK)

        def halves(ap):
            return ap.rearrange("p (a j) -> p a j", j=HALF)

        def scale_rows(t, lo, hi, diff):
            nc.vector.scalar_tensor_tensor(z_view[:, t, lo // HALF : hi // HALF, :], halves(diff), gain[:, t : t + 1], halves(h[t][:, lo:hi]), ALU.mult, ALU.mult)

        for t, width in ((0, S), (1, HALF)):
            same = new(f"same{t}", width, F32, tag="operand")
            diff = new(f"diff{t}", width, F32)
            nc.vector.tensor_copy(same[:], sg[t][:, :width])
            nc.vector.tensor_tensor(diff[:], sg[t][:].indirect(n2_t[:, : width // 16]), same[:], ALU.subtract)
            scale_rows(t, 0, width, diff[:])
        rest = ((2, 0), (3, 0), (1, 1), (2, 1), (3, 1))
        picked = new("picked", len(rest) * HALF, F32)
        diffs = new("diffs", len(rest) * HALF, F32, tag="operand")
        for i, (t, a) in enumerate(rest):
            nc.scalar.activation(picked[:, half(i)], sg[t][:].indirect(half_list(n2_t, a)), ACT.Copy)
            nc.vector.tensor_tensor(diffs[:, half(i)], picked[:, half(i)], sg[t][:, half(a)], ALU.subtract)
            scale_rows(t, a * HALF, (a + 1) * HALF, diffs[:, half(i)])

        def walk(ap):
            return ap.rearrange("p (c i) t -> p c t i", i=4)

        def quantise(name, rows, splits):
            codes = new(f"{name}_codes", S, U32)
            plane = new(f"{name}_plane", S, U8)
            woven = [new(f"{name}_woven{a}", PACK * HALF, BF16) for a in range(2)]
            for a in range(2):
                src = rows[a]
                dst = woven[a][:].rearrange("p (j t) -> p j t", t=PACK)
                cut = splits[a]
                if cut > 0:
                    nc.vector.tensor_copy(walk(dst[:, :cut, :]), walk(src[:, :cut, :]))
                if cut < HALF:
                    nc.scalar.copy(walk(dst[:, cut:, :]), walk(src[:, cut:, :]))
            for a in range(2):
                nc.vector.quantize_mx(codes[:, half(a)].bitcast(FP8X4), plane[:, half(a)], woven[a][:])
            return codes, plane

        z_codes, z_plane = quantise("z", [z_rows[:, a * PACK * HALF : (a + 1) * PACK * HALF].rearrange("p (t j) -> p j t", t=PACK) for a in range(2)], (0, 160))

        h2 = [new(f"h2{t}", S, F32, tag=f"row{t}") for t in range(PACK)]
        banks = {}
        for t in range(PACK):
            for a in range(2):
                bank = ps.tile([P, HALF], F32, name=f"h2_bank{t}{a}", tag=f"bank{t}{a}")
                banks[t, a] = bank
                nc.tensor.matmul_mx(
                    out=bank[:], lhsT=w_codes[:, 2 * t * P : 2 * (t + 1) * P].bitcast(FP4X4), lhsT_scale=w_plane[:, t * P : (t + 1) * P],
                    rhs=z_codes[:, half(a)].bitcast(FP8X4), rhs_scale=z_plane[:, half(a)], start=True, stop=True)

        npa = [new(f"npa{t}", HALF, F32) for t in range(PACK)]
        pb = [new(f"pb{t}", HALF, F32) for t in range(PACK)]
        rb = [new(f"rb{t}", HALF, F32) for t in range(PACK)]
        res = {}
        y_rows = new("y_rows", PACK * S, BF16)
        out_rows = out_0.rearrange("(p t) j -> p t j", t=PACK)

        def fetch(t):
            nc.scalar.copy(h2[t][:, half(0)], banks[t, 0][:])
            if t == 0:
                nc.vector.tensor_copy(h2[t][:, half(1)], banks[t, 1][:])
            else:
                nc.scalar.copy(h2[t][:, half(1)], banks[t, 1][:])
            nc.scalar.activation(npa[t][:], h2[t][:].indirect(n3_t[:]), ACT.Copy, scale=-1.0)
            if t < 3:
                nc.vector.tensor_copy(pb[t][:], h2[t][:].indirect(n4_t[:]))
            else:
                nc.scalar.activation(pb[t][:], h2[t][:].indirect(n4_t[:]), ACT.Copy)
            nc.vector.scalar_tensor_tensor(rb[t][:], npa[t][:], -0.5, pb[t][:], ALU.mult, ALU.max)

        def put_a(t):
            nc.vector.tensor_tensor(res[t][:].indirect(n3_t[:]), pb[t][:], npa[t][:], ALU.add)

        def put_b(t):
            nc.scalar.activation(res[t][:].indirect(n4_t[:]), rb[t][:], ACT.Copy)

        def finish(t):
            nc.sync.dma_start(out_rows[:, t, :], res[t][:])
            if t < 3:
                nc.vector.tensor_copy(y_rows[:, t * S : (t + 1) * S], res[t][:])
            else:
                nc.vector.tensor_copy(y_rows[:, t * S : t * S + HALF], res[t][:, half(0)])
                nc.scalar.copy(y_rows[:, t * S + HALF : (t + 1) * S], res[t][:, half(1)])

        for t in range(PACK):
            fetch(t)
        for t, slot in enumerate(("row2", "row0", "row1", "npa0")):
            res[t] = new(f"res{t}", S, F32, tag=slot)
        put_a(0)
        put_b(1)
        put_a(3)
        put_b(2)
        put_a(1)
        put_b(0)
        put_a(2)
        put_b(3)
        for t in (1, 0, 2, 3):
            finish(t)

        y_codes, y_plane = quantise("y", [y_rows[:].rearrange("p (t j) -> p j t", t=PACK)[:, half(a), :] for a in range(2)], (HALF, 96))
        words_out = out_1[0].rearrange("p c r -> p (c r)").bitcast(I32)
        for a in range(2):
            nc.sync.dma_start(words_out[:, half(a)], y_codes[:, half(a)].bitcast(I32))
        for q in range(4):
            eng = nc.scalar if q % 2 else nc.sync
            eng.dma_start(out_2[0, 4 * q : 4 * q + 4, :].bitcast(I32), y_plane[32 * q : 32 * q + 4, :].bitcast(I32))
